import numpy as np
import ml_dtypes


def mxq(x, axis, fmt="e4m3"):
    dtype, down = {"e4m3": (ml_dtypes.float8_e4m3fn, 7), "e5m2": (ml_dtypes.float8_e5m2, 14)}[fmt]
    v = np.moveaxis(np.asarray(x, np.float32).astype(ml_dtypes.bfloat16).astype(np.float64), axis, -1)
    blocks = v.reshape(v.shape[:-1] + (-1, 32))
    amax = np.abs(blocks).max(-1, keepdims=True)
    byte = np.maximum(np.where(amax > 0, np.frexp(amax)[1] - 1 + 127, 0) - down, 1)
    scale = np.exp2(byte - 127.0)
    codes = (blocks / scale).astype(np.float32).astype(dtype).astype(np.float64)
    return np.moveaxis((codes * scale).reshape(v.shape), -1, axis)


WIDE = False


def mx_kscale(k):
    if not WIDE:
        return np.ones(k)
    levels = np.array([10, -10, 5, -5, 0])
    if k % 512:
        return np.exp2(np.random.permutation(np.resize(levels, k // 32))).repeat(32)
    a = np.empty((k // 512, 16))
    for p in range(k // 512):
        a[p, :8] = np.random.permutation(np.resize(levels, 8))
        for g in range(8):
            far = levels[np.abs(levels - a[p, g]) >= 10]
            a[p, g + 8] = far[np.random.randint(len(far))]
    return np.exp2(a.ravel()).repeat(32)


def f64(x):
    return np.asarray(x).astype(np.float64)


def striped(idx):
    return np.tile(idx.reshape(-1, 16).T, (8, 1)).astype(np.uint16)


def unstriped(offs):
    return offs[:16].T.reshape(-1).astype(np.int64)


E2M1 = np.array([0.0, 0.5, 1.0, 1.5, 2.0, 3.0, 4.0, 6.0, -0.0, -0.5, -1.0, -1.5, -2.0, -3.0, -4.0, -6.0])


def pack_weight(w, fmt):
    k, n = w.shape
    w = f64(np.asarray(w, np.float32).astype(ml_dtypes.bfloat16)).reshape(k // 32, 32, n)
    amax = np.abs(w).max(1)
    if fmt == "e4m3":
        byte = np.frexp(amax)[1] - 1 + 127 - 7
    else:
        mant, ex = np.frexp(amax / 6.0)
        byte = np.where(mant > 0.5, ex, ex - 1) + 127
    byte = np.clip(np.where(amax > 0, byte, 1), 1, 254)
    scaled = (w * np.exp2(127.0 - byte)[:, None, :]).reshape(k, n).astype(np.float32)
    by_word = np.ascontiguousarray(scaled.reshape(k // 512, 128, 4, n).transpose(0, 1, 3, 2))
    if fmt == "e4m3":
        words = by_word.astype(ml_dtypes.float8_e4m3fn).view(np.uint8)
    else:
        c = by_word.astype(ml_dtypes.float4_e2m1fn).view(np.uint8) & 0xF
        words = (c[..., 0::2] | (c[..., 1::2] << 4)).reshape(k // 512, 128, 2 * n)
    return np.ascontiguousarray(words), np.ascontiguousarray(byte.astype(np.uint8).reshape(k // 512, 16, n))


def unpack_weight(words, scales, fmt):
    g, _, n = scales.shape
    words = np.ascontiguousarray(words).reshape(g, 128, n, -1)
    if fmt == "e4m3":
        vals = words.view(ml_dtypes.float8_e4m3fn).astype(np.float64)
    else:
        nib = np.empty((g, 128, n, 4), np.uint8)
        nib[..., 0::2] = words & 0xF
        nib[..., 1::2] = words >> 4
        vals = E2M1[nib]
    vals = vals * np.repeat(np.exp2(scales.astype(np.float64) - 127.0), 8, axis=1)[..., None]
    return vals.transpose(0, 1, 3, 2).reshape(g * 512, n)


def gelu(v):
    return 0.5 * v * (1.0 + np.tanh(np.sqrt(2.0 / np.pi) * (v + 0.044715 * v**3)))


def striped8(idx):
    return np.concatenate([v.reshape(-1, 16).T for v in idx]).astype(np.uint16)


def unstriped8(offs):
    return np.stack([offs[16 * g:16 * g + 16].T.reshape(-1) for g in range(8)]).astype(np.int64)


def put_heads(h, wgs, idx8, t2):
    r = np.arange(h.shape[0])
    page = np.zeros((h.shape[0], t2))
    page[r[:, None], idx8[r % 512 // 64]] = wgs[r // 4 % 128] * h
    return page


K, H, N, T, S, T2, P = 1024, 1024, 512, 2048, 512, 1024, 512


def setup_inputs():
    n = np.random.standard_normal
    s = mx_kscale(K)[:, None]
    u = mx_kscale(H)[:, None]
    tab_words, tab_scales = pack_weight(n((K, T)) * s, "e4m3")
    w4_words, w4_scales = pack_weight(1.5 * n((H, N)) / np.sqrt(H) / u, "e2m1")
    return {
        "tab_words": tab_words,
        "tab_scales": tab_scales,
        "offs": striped(np.random.permutation(T)[:S]),
        "w1": (0.53 * n((K, H)) / np.sqrt(K) / s).astype(np.float32),
        "gain": (1.7 * np.exp(0.3 * n(H))).astype(np.float32),
        "wgs": np.repeat(np.random.uniform(0.5, 2.0, (8, S)), 16, axis=0).astype(np.float32),
        "offs2": striped8(np.stack([np.random.permutation(T2)[:S] for _ in range(8)])),
        "offs3": striped(np.random.permutation(T2)[:P]),
        "timing": (0.8 * n((H, P)) * u).astype(np.float32),
        "w2": (1.5 * n((H, N)) / np.sqrt(H) / u).astype(np.float32),
        "w4_words": w4_words,
        "w4_scales": w4_scales,
        "level": np.exp(0.4 * n(N)).astype(np.float32),
    }


def reference(tab_words, tab_scales, offs, w1, gain, wgs, offs2, offs3, timing, w2, w4_words, w4_scales, level):
    v = unpack_weight(tab_words, tab_scales, "e4m3")[:, unstriped(offs)]
    w4 = unpack_weight(w4_words, w4_scales, "e2m1")
    h = np.sin(mxq(f64(w1), 0, "e4m3").T @ v) * f64(gain)[:, None]
    page = put_heads(h, f64(wgs), unstriped8(offs2), T2)
    x = page[:, unstriped(offs3)]
    tm = f64(timing)
    z = mxq(np.tanh(x + tm) * tm, 0, "e4m3")
    y2 = mxq(f64(w2), 0, "e4m3").T @ z
    y4 = w4.T @ z
    return np.maximum(y2, y4) * f64(level)[:, None]

@@ -1,0 +1,273 @@
+import math
+from contextlib import ExitStack
+
+import concourse.mybir as mybir
+from concourse.masks import make_identity
+
+K, H, N, T, S, T2, M = 1024, 1024, 512, 2048, 512, 1024, 512
+FLOPS = 2 * K * H * S + 2 * 2 * H * N * M
+
+F32 = mybir.dt.float32
+BF16 = mybir.dt.bfloat16
+I32 = mybir.dt.int32
+U32 = mybir.dt.uint32
+U16 = mybir.dt.uint16
+U8 = mybir.dt.uint8
+FP8X4 = mybir.dt.float8_e4m3fn_x4
+FP4X4 = mybir.dt.float4_e2m1fn_x4
+ACT = mybir.ActivationFunctionType
+ALU = mybir.AluOpType
+
+P = 128
+PACK = 4
+PASS = P * PACK
+HALF = M // 2
+TURN = 2.0 * math.pi
+ROUNDER = 1.5 * 2.0**23
+
+
+def tile_list_garble_pulse_scores_kernel(
+    tc, tab_words, tab_scales, offs, w1, gain, wgs, offs2, offs3, timing, w2, w4_words, w4_scales, level, out
+):
+    nc = tc.nc
+    with ExitStack() as ctx:
+        keep = ctx.enter_context(tc.tile_pool(name="keep", bufs=1))
+        psum = ctx.enter_context(tc.psum_pool(name="psum", bufs=1))
+
+        def load_rows(src, name, tag, bufs):
+            raw = keep.tile([P, PACK, PASS], F32, name=name, tag=tag, bufs=bufs)
+            nc.sync.dma_start(out=raw[:], in_=src.rearrange("(p j) c -> p j c", j=PACK))
+            return raw
+
+        idx1 = keep.tile([P, S // 16], U16, name="idx1")
+        idx2 = keep.tile([P, S // 16], U16, name="idx2")
+        idx3 = keep.tile([P, M // 16], U16, name="idx3")
+        tab_sc = keep.tile([P, T], U8, name="tab_sc", align_bytes=64)
+        nc.vector.memset(tab_sc[:].bitcast(I32), 0)
+        w4_sc = keep.tile([P, 2, N], U8, name="w4_sc", align_bytes=64)
+        nc.vector.memset(w4_sc[:].bitcast(I32), 0)
+        pages = [keep.tile([P, T2], F32, name="page%d" % i) for i in range(2)]
+        for page in pages:
+            nc.gpsimd.memset(page[:], 0.0)
+
+        ident = keep.tile([P, P], F32, name="ident")
+        make_identity(nc, ident[:])
+        tab_w = [keep.tile([P, T], I32, name="tab_w%d" % a) for a in range(2)]
+
+        def load_table(a):
+            nc.sync.dma_start(out=tab_w[a][:], in_=tab_words[a].rearrange("p t i -> p (t i)").bitcast(I32))
+
+        w1_raw = {}
+
+        def load_w1(a, b):
+            w1_raw[a, b] = load_rows(
+                w1[a * PASS : (a + 1) * PASS, b * PASS : (b + 1) * PASS], "w1_raw%d%d" % (a, b), "raw", 4
+            )
+
+        nc.sync.dma_start(idx1[:], offs)
+        load_table(0)
+        for q in range(4):
+            nc.scalar.dma_start(
+                out=tab_sc[32 * q : 32 * q + 8, :].bitcast(I32), in_=tab_scales[:, 4 * q : 4 * q + 4, :].bitcast(I32)
+            )
+        load_w1(0, 0)
+        gain_sb = keep.tile([P, 2, PACK], F32, name="gain_sb")
+        nc.sync.dma_start(out=gain_sb[:], in_=gain.rearrange("(b p t) -> p b t", b=2, t=PACK))
+        nc.sync.dma_start(idx2[:], offs2)
+        load_w1(1, 0)
+        load_table(1)
+        wgs_sb = keep.tile([P, S], F32, name="wgs_sb")
+        nc.sync.dma_start(out=wgs_sb[:], in_=wgs)
+        nc.sync.dma_start(idx3[:], offs3)
+        tm = [None, None]
+        tm[0] = load_rows(timing[0:PASS, :], "tm0", "tm", 2)
+        load_w1(0, 1)
+        load_w1(1, 1)
+        tm[1] = load_rows(timing[PASS:H, :], "tm1", "tm", 2)
+        w2_raw = [load_rows(w2[b * PASS : (b + 1) * PASS, :], "w2_raw%d" % b, "raw", 4) for b in range(2)]
+        w4_w = keep.tile([P, 2, 2 * N], U8, name="w4_w", align_bytes=64)
+        nc.sync.dma_start(out=w4_w[:].bitcast(I32), in_=w4_words.rearrange("a p c -> p a c").bitcast(I32))
+        for q in range(4):
+            nc.sync.dma_start(
+                out=w4_sc[32 * q : 32 * q + 4, :, :].bitcast(I32),
+                in_=w4_scales[:, 4 * q : 4 * q + 4, :].rearrange("a r n -> r a n").bitcast(I32),
+            )
+        level_sb = keep.tile([P, N // P], F32, name="level_sb")
+        with nc.allow_non_contiguous_dma(reason="one value of level to a partition"):
+            nc.sync.dma_start(out=level_sb[:], in_=level.rearrange("(c p) -> p c", p=P))
+
+        v_w = [keep.tile([P, S], U32, name="v_w%d" % a, align_bytes=64) for a in range(2)]
+        v_sc = keep.tile([P, S], U8, name="v_sc", align_bytes=64)
+
+        def entries(cols):
+            return slice(cols.start // 16, cols.stop // 16)
+
+        def gather_table(a, cols):
+            nc.vector.tensor_copy(v_w[a][:, cols], tab_w[a][:].bitcast(U32).indirect(idx1[:, entries(cols)]))
+
+        def quantize(rounded, name, width):
+            codes = keep.tile([P, width], U32, name=name + "_w", align_bytes=64)
+            scales = keep.tile([P, width], U8, name=name + "_sc", align_bytes=64)
+            nc.vector.quantize_mx(out=codes[:].bitcast(FP8X4), scales=scales[:], in_=rounded[:])
+            return codes, scales
+
+        w1_q = {}
+
+        def quantize_w1(a, b, vector_cols):
+            rounded = keep.tile([P, PACK * PASS], BF16, name="w1_bf%d%d" % (a, b), tag="bf", bufs=4, align_bytes=64)
+            dst = rounded[:].rearrange("p (t m j) -> p m j t", t=PACK, j=PACK)
+            src = w1_raw[a, b][:].rearrange("p j (m t) -> p m j t", t=PACK)
+            if vector_cols:
+                nc.vector.tensor_copy(out=dst[:, :vector_cols], in_=src[:, :vector_cols])
+                nc.scalar.copy(out=dst[:, vector_cols:], in_=src[:, vector_cols:])
+            else:
+                for m0 in range(0, P, P // 2):
+                    nc.scalar.copy(out=dst[:, m0 : m0 + P // 2], in_=src[:, m0 : m0 + P // 2])
+            w1_q[a, b] = quantize(rounded, "w1_%d%d" % (a, b), PASS)
+
+        whole, halves = slice(0, S), [slice(0, HALF), slice(HALF, S)]
+        gather_table(0, whole)
+        nc.vector.tensor_copy(v_sc[:], tab_sc[:].indirect(idx1[:]))
+        quantize_w1(0, 0, 0)
+        quantize_w1(1, 0, 80)
+
+        sines = [keep.tile([P, S], F32, name="sine%d" % s, tag="line%d" % s) for s in range(8)]
+        wg = [keep.tile([P, S], F32, name="wg%d" % s) for s in range(8)]
+        for s in range(8):
+            nc.gpsimd.tensor_scalar(wg[s][:], wgs_sb[:], gain_sb[:, s // PACK, s % PACK : s % PACK + 1], 0.0, ALU.mult, ALU.add)
+
+        def first_stage(s, js, bank):
+            b, t = divmod(s, PACK)
+            cols = slice(t * P, (t + 1) * P)
+            width = js.stop - js.start
+            blocks = [slice(c, c + P) for c in range(0, width, P)]
+            acc = psum.tile([P, width], F32, name="acc", tag="bank%d" % bank)
+            for block in blocks:
+                picked = slice(js.start + block.start, js.start + block.stop)
+                for a in range(2):
+                    codes, scales = w1_q[a, b]
+                    nc.tensor.matmul_mx(
+                        out=acc[:, block], lhsT=v_w[a][:, picked].bitcast(FP8X4), lhsT_scale=v_sc[4 * a :, picked],
+                        rhs=codes[:, cols].bitcast(FP8X4), rhs_scale=scales[:, cols], start=(a == 0), stop=(a == 1),
+                    )
+            shifted = keep.tile([P, width], U32, name="shifted", bufs=2)
+            nc.scalar.activation(shifted[:], acc[:], ACT.Copy, bias=ROUNDER, scale=1.0 / TURN)
+            turns = keep.tile([P, width], F32, name="turns", bufs=2)
+            nc.scalar.activation(turns[:], acc[:], ACT.Copy, bias=0.0, scale=1.0 / TURN)
+            if s == 7:
+                whole_turns = keep.tile([P, width], F32, name="last_whole_turns", tag="th0")
+            else:
+                whole_turns = keep.tile([P, width], F32, name="whole_turns", bufs=2)
+            nc.scalar.activation(whole_turns[:], shifted[:], ACT.Copy, bias=ROUNDER, scale=-1.0)
+            rest = psum.tile([P, width], F32, name="rest", tag="bank%d" % (4 + bank))
+            for block in blocks:
+                nc.tensor.matmul(rest[:, block], lhsT=turns[:, block], rhs=ident[:], is_transpose=True, start=True, stop=False)
+                nc.tensor.matmul(rest[:, block], lhsT=whole_turns[:, block], rhs=ident[:], is_transpose=True, start=False, stop=True)
+            nc.scalar.activation(sines[s][:, js], rest[:], ACT.Sin, scale=TURN)
+
+        th = {}
+
+        def put(s, js):
+            nc.vector.tensor_tensor(
+                pages[s % 2][:].indirect(idx2[:, entries(js)]), sines[s][:, js], wg[s][:, js], ALU.mult
+            )
+
+        def fetch(s, pieces):
+            b, t = divmod(s, PACK)
+            width = M // pieces
+            summed = keep.tile([P, M], F32, name="summed%d" % s, tag="line%d" % ((s + 1) % 8))
+            for c in range(pieces):
+                cols = slice(c * width, (c + 1) * width)
+                nc.vector.tensor_tensor(
+                    summed[:, cols],
+                    pages[s % 2][:].indirect(idx3[:, c * width // 16 : (c + 1) * width // 16]),
+                    tm[b][:, t, cols],
+                    ALU.add,
+                )
+            if t == 0:
+                th[b] = keep.tile([P, 2, PACK, HALF], F32, name="th%d" % b, tag="th%d" % b)
+            for h in range(2):
+                nc.scalar.activation(th[b][:, h, t, :], summed[:, h * HALF : (h + 1) * HALF], ACT.Tanh)
+
+        w2_q = {}
+
+        def quantize_w2(b):
+            rounded = keep.tile([P, PACK * N], BF16, name="w2_bf%d" % b, tag="bf", bufs=4, align_bytes=64)
+            nc.scalar.copy(
+                out=rounded[:].rearrange("p (c i j) -> p c j i", i=4, j=PACK),
+                in_=w2_raw[b][:].rearrange("p j (c i) -> p c j i", i=4),
+            )
+            w2_q[b] = quantize(rounded, "w2_%d" % b, N)
+
+        z_q = {}
+
+        def make_z(b, h):
+            z = keep.tile([P, PACK * HALF], BF16, name="z%d%d" % (b, h), align_bytes=64)
+            nc.vector.tensor_tensor(
+                z[:].rearrange("p (c i t) -> p c t i", i=4, t=PACK),
+                th[b][:, h].rearrange("p t (c i) -> p c t i", i=4),
+                tm[b][:, :, h * HALF : (h + 1) * HALF].rearrange("p t (c i) -> p c t i", i=4),
+                ALU.mult,
+            )
+            z_q[b, h] = quantize(z, "z_%d%d" % (b, h), HALF)
+
+        banks = {}
+
+        def second_stage(b, h):
+            z_w, z_sc = z_q[b, h]
+            for c in range(N // P):
+                if b == 0:
+                    banks[h, c] = psum.tile([P, 2, HALF], F32, name="y%d%d" % (h, c), tag="bank%d" % (4 * h + c))
+                cols = slice(c * P, (c + 1) * P)
+                codes, scales = w2_q[b]
+                nc.tensor.matmul_mx(
+                    out=banks[h, c][:, 0, :], lhsT=codes[:, cols].bitcast(FP8X4), lhsT_scale=scales[:, cols],
+                    rhs=z_w[:].bitcast(FP8X4), rhs_scale=z_sc[:], start=(b == 0), stop=False,
+                )
+                nc.tensor.matmul_mx(
+                    out=banks[h, c][:, 1, :],
+                    lhsT=w4_w[:, b, 2 * c * P : 2 * (c + 1) * P].bitcast(FP4X4), lhsT_scale=w4_sc[:, b, cols],
+                    rhs=z_w[:].bitcast(FP8X4), rhs_scale=z_sc[:], start=False, stop=(b == 1),
+                )
+
+        def finish(h):
+            scored = keep.tile([P, N // P, HALF], F32, name="scored%d" % h)
+            for c in range(N // P):
+                y4 = keep.tile([P, HALF], F32, name="y4", bufs=4)
+                nc.scalar.copy(out=y4[:], in_=banks[h, c][:, 1, :])
+                larger = keep.tile([P, HALF], F32, name="larger", bufs=4)
+                nc.vector.tensor_tensor(larger[:], banks[h, c][:, 0, :], y4[:], ALU.max)
+                nc.scalar.activation(scored[:, c, :], larger[:], ACT.Copy, scale=level_sb[:, c : c + 1])
+                if c % 2:
+                    nc.sync.dma_start(
+                        out=out[(c - 1) * P : (c + 1) * P, h * HALF : (h + 1) * HALF].rearrange("(c p) m -> p c m", p=P),
+                        in_=scored[:, c - 1 : c + 1, :],
+                    )
+
+        for h in range(2):
+            gather_table(1, halves[h])
+        for h in range(2):
+            first_stage(0, halves[h], h)
+            put(0, halves[h])
+        first_stage(1, whole, 2)
+        put(1, whole)
+        quantize_w1(0, 1, 0)
+        quantize_w1(1, 1, 0)
+        for s in range(2, 8):
+            first_stage(s, whole, (s + 1) % 4)
+        fetch(0, 1)
+        for s in range(2, 8):
+            put(s, whole)
+            fetch(s - 1, 1)
+            if s == 3:
+                quantize_w2(0)
+                quantize_w2(1)
+            if s == 5:
+                for h in range(2):
+                    make_z(0, h)
+                    second_stage(0, h)
+        fetch(7, 2)
+        for h in range(2):
+            make_z(1, h)
+            second_stage(1, h)
+            finish(h)

@@ -1,3 +1,4 @@
+import itertools
 import math
 from contextlib import ExitStack
 
@@ -22,6 +23,7 @@ P = 128
 PACK = 4
 PASS = P * PACK
 HALF = M // 2
+RING = 3
 TURN = 2.0 * math.pi
 ROUNDER = 1.5 * 2.0**23
 
@@ -43,13 +45,15 @@ def tile_list_garble_pulse_scores_kernel(
         idx2 = keep.tile([P, S // 16], U16, name="idx2")
         idx3 = keep.tile([P, M // 16], U16, name="idx3")
         tab_sc = keep.tile([P, T], U8, name="tab_sc", align_bytes=64)
-        nc.vector.memset(tab_sc[:].bitcast(I32), 0)
+        nc.gpsimd.memset(tab_sc[:].bitcast(I32), 0)
         w4_sc = keep.tile([P, 2, N], U8, name="w4_sc", align_bytes=64)
         nc.vector.memset(w4_sc[:].bitcast(I32), 0)
         pages = [keep.tile([P, T2], F32, name="page%d" % i) for i in range(2)]
         for page in pages:
-            nc.gpsimd.memset(page[:], 0.0)
+            nc.vector.memset(page[:], 0.0)
 
+        warm = keep.tile([P, 1], F32, name="warm")
+        nc.scalar.activation(warm[:], pages[0][:, 0:1], ACT.Silu)
         ident = keep.tile([P, P], F32, name="ident")
         make_identity(nc, ident[:])
         tab_w = [keep.tile([P, T], I32, name="tab_w%d" % a) for a in range(2)]
@@ -65,24 +69,24 @@ def tile_list_garble_pulse_scores_kernel(
             )
 
         nc.sync.dma_start(idx1[:], offs)
-        load_table(0)
+        load_w1(0, 0)
         for q in range(4):
-            nc.scalar.dma_start(
+            nc.sync.dma_start(
                 out=tab_sc[32 * q : 32 * q + 8, :].bitcast(I32), in_=tab_scales[:, 4 * q : 4 * q + 4, :].bitcast(I32)
             )
-        load_w1(0, 0)
-        gain_sb = keep.tile([P, 2, PACK], F32, name="gain_sb")
-        nc.sync.dma_start(out=gain_sb[:], in_=gain.rearrange("(b p t) -> p b t", b=2, t=PACK))
-        nc.sync.dma_start(idx2[:], offs2)
         load_w1(1, 0)
+        load_table(0)
         load_table(1)
         wgs_sb = keep.tile([P, S], F32, name="wgs_sb")
         nc.sync.dma_start(out=wgs_sb[:], in_=wgs)
+        gain_sb = keep.tile([P, 2, PACK], F32, name="gain_sb")
+        nc.sync.dma_start(out=gain_sb[:], in_=gain.rearrange("(b p t) -> p b t", b=2, t=PACK))
+        nc.sync.dma_start(idx2[:], offs2)
         nc.sync.dma_start(idx3[:], offs3)
         tm = [None, None]
-        tm[0] = load_rows(timing[0:PASS, :], "tm0", "tm", 2)
         load_w1(0, 1)
         load_w1(1, 1)
+        tm[0] = load_rows(timing[0:PASS, :], "tm0", "tm", 2)
         tm[1] = load_rows(timing[PASS:H, :], "tm1", "tm", 2)
         w2_raw = [load_rows(w2[b * PASS : (b + 1) * PASS, :], "w2_raw%d" % b, "raw", 4) for b in range(2)]
         w4_w = keep.tile([P, 2, 2 * N], U8, name="w4_w", align_bytes=64)
@@ -119,29 +123,37 @@ def tile_list_garble_pulse_scores_kernel(
             src = w1_raw[a, b][:].rearrange("p j (m t) -> p m j t", t=PACK)
             if vector_cols:
                 nc.vector.tensor_copy(out=dst[:, :vector_cols], in_=src[:, :vector_cols])
-                nc.scalar.copy(out=dst[:, vector_cols:], in_=src[:, vector_cols:])
+                if vector_cols < P:
+                    nc.scalar.copy(out=dst[:, vector_cols:], in_=src[:, vector_cols:])
             else:
-                for m0 in range(0, P, P // 2):
-                    nc.scalar.copy(out=dst[:, m0 : m0 + P // 2], in_=src[:, m0 : m0 + P // 2])
+                for m0 in range(0, P, P // 4):
+                    nc.scalar.copy(out=dst[:, m0 : m0 + P // 4], in_=src[:, m0 : m0 + P // 4])
             w1_q[a, b] = quantize(rounded, "w1_%d%d" % (a, b), PASS)
 
         whole, halves = slice(0, S), [slice(0, HALF), slice(HALF, S)]
-        gather_table(0, whole)
         nc.vector.tensor_copy(v_sc[:], tab_sc[:].indirect(idx1[:]))
         quantize_w1(0, 0, 0)
-        quantize_w1(1, 0, 80)
+        quantize_w1(1, 0, 0)
+        gather_table(0, whole)
 
         sines = [keep.tile([P, S], F32, name="sine%d" % s, tag="line%d" % s) for s in range(8)]
         wg = [keep.tile([P, S], F32, name="wg%d" % s) for s in range(8)]
         for s in range(8):
             nc.gpsimd.tensor_scalar(wg[s][:], wgs_sb[:], gain_sb[:, s // PACK, s % PACK : s % PACK + 1], 0.0, ALU.mult, ALU.add)
 
-        def first_stage(s, js, bank):
+        taken = []
+
+        def ring_bank(name, width):
+            taken.append(name)
+            bank = len(taken) % RING
+            return psum.tile([P, width], F32, name=name, tag="bank%d" % bank)
+
+        def first_stage(s, js):
             b, t = divmod(s, PACK)
             cols = slice(t * P, (t + 1) * P)
             width = js.stop - js.start
             blocks = [slice(c, c + P) for c in range(0, width, P)]
-            acc = psum.tile([P, width], F32, name="acc", tag="bank%d" % bank)
+            acc = ring_bank("acc", width)
             for block in blocks:
                 picked = slice(js.start + block.start, js.start + block.stop)
                 for a in range(2):
@@ -154,16 +166,32 @@ def tile_list_garble_pulse_scores_kernel(
             nc.scalar.activation(shifted[:], acc[:], ACT.Copy, bias=ROUNDER, scale=1.0 / TURN)
             turns = keep.tile([P, width], F32, name="turns", bufs=2)
             nc.scalar.activation(turns[:], acc[:], ACT.Copy, bias=0.0, scale=1.0 / TURN)
-            if s == 7:
-                whole_turns = keep.tile([P, width], F32, name="last_whole_turns", tag="th0")
-            else:
-                whole_turns = keep.tile([P, width], F32, name="whole_turns", bufs=2)
+            whole_turns = keep.tile([P, width], F32, name="whole_turns", bufs=2)
             nc.scalar.activation(whole_turns[:], shifted[:], ACT.Copy, bias=ROUNDER, scale=-1.0)
-            rest = psum.tile([P, width], F32, name="rest", tag="bank%d" % (4 + bank))
-            for block in blocks:
-                nc.tensor.matmul(rest[:, block], lhsT=turns[:, block], rhs=ident[:], is_transpose=True, start=True, stop=False)
-                nc.tensor.matmul(rest[:, block], lhsT=whole_turns[:, block], rhs=ident[:], is_transpose=True, start=False, stop=True)
+            rest = ring_bank("rest", width)
+            for i, (term, block) in enumerate(itertools.product((turns, whole_turns), blocks)):
+                nc.tensor.matmul(
+                    rest[:, block], lhsT=term[:, block], rhs=ident[:], is_transpose=True,
+                    start=(i == 0), stop=(i == 2 * len(blocks) - 1),
+                )
             nc.scalar.activation(sines[s][:, js], rest[:], ACT.Sin, scale=TURN)
+
+        def first_stage_head(js):
+            width = js.stop - js.start
+            acc = ring_bank("acc", width)
+            for a in range(2):
+                codes, scales = w1_q[a, 0]
+                nc.tensor.matmul_mx(
+                    out=acc[:], lhsT=codes[:, 0:P].bitcast(FP8X4), lhsT_scale=scales[:, 0:P],
+                    rhs=v_w[a][:, js].bitcast(FP8X4), rhs_scale=v_sc[4 * a :, js], start=(a == 0), stop=(a == 1),
+                )
+            shifted = keep.tile([P, width], U32, name="shifted", bufs=2)
+            nc.scalar.activation(shifted[:], acc[:], ACT.Copy, bias=ROUNDER, scale=1.0 / TURN)
+            whole_turns = keep.tile([P, width], F32, name="whole_turns", bufs=2)
+            nc.scalar.activation(whole_turns[:], shifted[:], ACT.Copy, bias=ROUNDER, scale=-1.0)
+            angle = keep.tile([P, width], F32, name="angle", bufs=2)
+            nc.vector.scalar_tensor_tensor(angle[:], whole_turns[:], TURN, acc[:], ALU.mult, ALU.add)
+            nc.scalar.activation(sines[0][:, js], angle[:], ACT.Sin)
 
         th = {}
 
@@ -235,7 +263,7 @@ def tile_list_garble_pulse_scores_kernel(
             for c in range(N // P):
                 y4 = keep.tile([P, HALF], F32, name="y4", bufs=4)
                 nc.scalar.copy(out=y4[:], in_=banks[h, c][:, 1, :])
-                larger = keep.tile([P, HALF], F32, name="larger", bufs=4)
+                larger = keep.tile([P, HALF], F32, name="larger", bufs=8)
                 nc.vector.tensor_tensor(larger[:], banks[h, c][:, 0, :], y4[:], ALU.max)
                 nc.scalar.activation(scored[:, c, :], larger[:], ACT.Copy, scale=level_sb[:, c : c + 1])
                 if c % 2:
@@ -246,23 +274,25 @@ def tile_list_garble_pulse_scores_kernel(
 
         for h in range(2):
             gather_table(1, halves[h])
-        for h in range(2):
-            first_stage(0, halves[h], h)
-            put(0, halves[h])
-        first_stage(1, whole, 2)
+        for js in halves:
+            first_stage_head(js)
+        for js in halves:
+            put(0, js)
+        taken.append("skip")
+        first_stage(1, whole)
         put(1, whole)
         quantize_w1(0, 1, 0)
         quantize_w1(1, 1, 0)
         for s in range(2, 8):
-            first_stage(s, whole, (s + 1) % 4)
+            first_stage(s, whole)
         fetch(0, 1)
         for s in range(2, 8):
             put(s, whole)
             fetch(s - 1, 1)
-            if s == 3:
+            if s == 2:
                 quantize_w2(0)
                 quantize_w2(1)
-            if s == 5:
+            if s == 4:
                 for h in range(2):
                     make_z(0, h)
                     second_stage(0, h)
@@ -270,4 +300,5 @@ def tile_list_garble_pulse_scores_kernel(
         for h in range(2):
             make_z(1, h)
             second_stage(1, h)
+        for h in range(2):
             finish(h)

@@ -109,8 +109,8 @@ def tile_list_garble_pulse_scores_kernel(
         def gather_table(a, cols):
             nc.vector.tensor_copy(v_w[a][:, cols], tab_w[a][:].bitcast(U32).indirect(idx1[:, entries(cols)]))
 
-        def quantize(rounded, name, width):
-            codes = keep.tile([P, width], U32, name=name + "_w", align_bytes=64)
+        def quantize(rounded, name, width, tag=None):
+            codes = keep.tile([P, width], U32, name=name + "_w", tag=tag or name + "_w", align_bytes=64)
             scales = keep.tile([P, width], U8, name=name + "_sc", align_bytes=64)
             nc.vector.quantize_mx(out=codes[:].bitcast(FP8X4), scales=scales[:], in_=rounded[:])
             return codes, scales
@@ -133,11 +133,11 @@ def tile_list_garble_pulse_scores_kernel(
         whole, halves = slice(0, S), [slice(0, HALF), slice(HALF, S)]
         nc.vector.tensor_copy(v_sc[:], tab_sc[:].indirect(idx1[:]))
         quantize_w1(0, 0, 0)
-        quantize_w1(1, 0, 0)
+        quantize_w1(1, 0, 64)
         gather_table(0, whole)
 
         sines = [keep.tile([P, S], F32, name="sine%d" % s, tag="line%d" % s) for s in range(8)]
-        wg = [keep.tile([P, S], F32, name="wg%d" % s) for s in range(8)]
+        wg = [keep.tile([P, S], F32, name="wg%d" % s, align_bytes=64) for s in range(8)]
         for s in range(8):
             nc.gpsimd.tensor_scalar(wg[s][:], wgs_sb[:], gain_sb[:, s // PACK, s % PACK : s % PACK + 1], 0.0, ALU.mult, ALU.add)
 
@@ -227,17 +227,20 @@ def tile_list_garble_pulse_scores_kernel(
             )
             w2_q[b] = quantize(rounded, "w2_%d" % b, N)
 
-        z_q = {}
+        z_bf, z_q = {}, {}
 
         def make_z(b, h):
-            z = keep.tile([P, PACK * HALF], BF16, name="z%d%d" % (b, h), align_bytes=64)
+            z = keep.tile([P, PACK * HALF], BF16, name="z%d%d" % (b, h), tag="z%d" % (h if b == 0 else 2), align_bytes=64)
             nc.vector.tensor_tensor(
-                z[:].rearrange("p (c i t) -> p c t i", i=4, t=PACK),
-                th[b][:, h].rearrange("p t (c i) -> p c t i", i=4),
-                tm[b][:, :, h * HALF : (h + 1) * HALF].rearrange("p t (c i) -> p c t i", i=4),
+                z[:].rearrange("p (c i t) -> p c t i", i=2, t=PACK),
+                th[b][:, h].rearrange("p t (c i) -> p c t i", i=2),
+                tm[b][:, :, h * HALF : (h + 1) * HALF].rearrange("p t (c i) -> p c t i", i=2),
                 ALU.mult,
             )
-            z_q[b, h] = quantize(z, "z_%d%d" % (b, h), HALF)
+            z_bf[b, h] = z
+
+        def quantize_z(b, h, tag=None):
+            z_q[b, h] = quantize(z_bf[b, h], "z_%d%d" % (b, h), HALF, tag)
 
         banks = {}
 
@@ -260,17 +263,19 @@ def tile_list_garble_pulse_scores_kernel(
 
         def finish(h):
             scored = keep.tile([P, N // P, HALF], F32, name="scored%d" % h)
+            best = []
             for c in range(N // P):
-                y4 = keep.tile([P, HALF], F32, name="y4", bufs=4)
+                y4 = keep.tile([P, HALF], F32, name="y4", bufs=8)
                 nc.scalar.copy(out=y4[:], in_=banks[h, c][:, 1, :])
                 larger = keep.tile([P, HALF], F32, name="larger", bufs=8)
                 nc.vector.tensor_tensor(larger[:], banks[h, c][:, 0, :], y4[:], ALU.max)
-                nc.scalar.activation(scored[:, c, :], larger[:], ACT.Copy, scale=level_sb[:, c : c + 1])
-                if c % 2:
-                    nc.sync.dma_start(
-                        out=out[(c - 1) * P : (c + 1) * P, h * HALF : (h + 1) * HALF].rearrange("(c p) m -> p c m", p=P),
-                        in_=scored[:, c - 1 : c + 1, :],
-                    )
+                best.append(larger)
+            for c, larger in enumerate(best):
+                if h == 0:
+                    nc.gpsimd.tensor_scalar(scored[:, c, :], larger[:], level_sb[:, c : c + 1], 0.0, ALU.mult, ALU.add)
+                else:
+                    nc.scalar.activation(scored[:, c, :], larger[:], ACT.Copy, scale=level_sb[:, c : c + 1])
+                nc.sync.dma_start(out=out[c * P : (c + 1) * P, halves[h]], in_=scored[:, c, :])
 
         for h in range(2):
             gather_table(1, halves[h])
@@ -278,16 +283,19 @@ def tile_list_garble_pulse_scores_kernel(
             first_stage_head(js)
         for js in halves:
             put(0, js)
-        taken.append("skip")
         first_stage(1, whole)
         put(1, whole)
-        quantize_w1(0, 1, 0)
+        quantize_w1(0, 1, 64)
         quantize_w1(1, 1, 0)
         for s in range(2, 8):
             first_stage(s, whole)
         fetch(0, 1)
         for s in range(2, 8):
             put(s, whole)
+            if s == 7:
+                for h in range(2):
+                    quantize_z(0, h, ("wg7", "z0")[h])
+                    second_stage(0, h)
             fetch(s - 1, 1)
             if s == 2:
                 quantize_w2(0)
@@ -295,10 +303,10 @@ def tile_list_garble_pulse_scores_kernel(
             if s == 4:
                 for h in range(2):
                     make_z(0, h)
-                    second_stage(0, h)
         fetch(7, 2)
         for h in range(2):
             make_z(1, h)
+            quantize_z(1, h)
             second_stage(1, h)
         for h in range(2):
             finish(h)

import itertools
import math
from contextlib import ExitStack

import concourse.mybir as mybir
from concourse.masks import make_identity

K, H, N, T, S, T2, M = 1024, 1024, 512, 2048, 512, 1024, 512
FLOPS = 2 * K * H * S + 2 * 2 * H * N * M

F32 = mybir.dt.float32
BF16 = mybir.dt.bfloat16
I32 = mybir.dt.int32
U32 = mybir.dt.uint32
U16 = mybir.dt.uint16
U8 = mybir.dt.uint8
FP8X4 = mybir.dt.float8_e4m3fn_x4
FP4X4 = mybir.dt.float4_e2m1fn_x4
ACT = mybir.ActivationFunctionType
ALU = mybir.AluOpType

P = 128
PACK = 4
PASS = P * PACK
HALF = M // 2
RING = 3
TURN = 2.0 * math.pi
ROUNDER = 1.5 * 2.0**23


def tile_list_garble_pulse_scores_kernel(
    tc, tab_words, tab_scales, offs, w1, gain, wgs, offs2, offs3, timing, w2, w4_words, w4_scales, level, out
):
    nc = tc.nc
    with ExitStack() as ctx:
        keep = ctx.enter_context(tc.tile_pool(name="keep", bufs=1))
        psum = ctx.enter_context(tc.psum_pool(name="psum", bufs=1))

        def load_rows(src, name, tag, bufs):
            raw = keep.tile([P, PACK, PASS], F32, name=name, tag=tag, bufs=bufs)
            nc.sync.dma_start(out=raw[:], in_=src.rearrange("(p j) c -> p j c", j=PACK))
            return raw

        idx1 = keep.tile([P, S // 16], U16, name="idx1")
        idx2 = keep.tile([P, S // 16], U16, name="idx2")
        idx3 = keep.tile([P, M // 16], U16, name="idx3")
        tab_sc = keep.tile([P, T], U8, name="tab_sc", align_bytes=64)
        nc.gpsimd.memset(tab_sc[:].bitcast(I32), 0)
        w4_sc = keep.tile([P, 2, N], U8, name="w4_sc", align_bytes=64)
        nc.vector.memset(w4_sc[:].bitcast(I32), 0)
        pages = [keep.tile([P, T2], F32, name="page%d" % i) for i in range(2)]
        for page in pages:
            nc.vector.memset(page[:], 0.0)

        warm = keep.tile([P, 1], F32, name="warm")
        nc.scalar.activation(warm[:], pages[0][:, 0:1], ACT.Silu)
        ident = keep.tile([P, P], F32, name="ident")
        make_identity(nc, ident[:])
        tab_w = [keep.tile([P, T], I32, name="tab_w%d" % a) for a in range(2)]

        def load_table(a):
            nc.sync.dma_start(out=tab_w[a][:], in_=tab_words[a].rearrange("p t i -> p (t i)").bitcast(I32))

        w1_raw = {}

        def load_w1(a, b):
            w1_raw[a, b] = load_rows(
                w1[a * PASS : (a + 1) * PASS, b * PASS : (b + 1) * PASS], "w1_raw%d%d" % (a, b), "raw", 4
            )

        nc.sync.dma_start(idx1[:], offs)
        load_w1(0, 0)
        for q in range(4):
            nc.sync.dma_start(
                out=tab_sc[32 * q : 32 * q + 8, :].bitcast(I32), in_=tab_scales[:, 4 * q : 4 * q + 4, :].bitcast(I32)
            )
        load_w1(1, 0)
        load_table(0)
        load_table(1)
        wgs_sb = keep.tile([P, S], F32, name="wgs_sb")
        nc.sync.dma_start(out=wgs_sb[:], in_=wgs)
        gain_sb = keep.tile([P, 2, PACK], F32, name="gain_sb")
        nc.sync.dma_start(out=gain_sb[:], in_=gain.rearrange("(b p t) -> p b t", b=2, t=PACK))
        nc.sync.dma_start(idx2[:], offs2)
        nc.sync.dma_start(idx3[:], offs3)
        tm = [None, None]
        load_w1(0, 1)
        load_w1(1, 1)
        tm[0] = load_rows(timing[0:PASS, :], "tm0", "tm", 2)
        tm[1] = load_rows(timing[PASS:H, :], "tm1", "tm", 2)
        w2_raw = [load_rows(w2[b * PASS : (b + 1) * PASS, :], "w2_raw%d" % b, "raw", 4) for b in range(2)]
        w4_w = keep.tile([P, 2, 2 * N], U8, name="w4_w", align_bytes=64)
        nc.sync.dma_start(out=w4_w[:].bitcast(I32), in_=w4_words.rearrange("a p c -> p a c").bitcast(I32))
        for q in range(4):
            nc.sync.dma_start(
                out=w4_sc[32 * q : 32 * q + 4, :, :].bitcast(I32),
                in_=w4_scales[:, 4 * q : 4 * q + 4, :].rearrange("a r n -> r a n").bitcast(I32),
            )
        level_sb = keep.tile([P, N // P], F32, name="level_sb")
        with nc.allow_non_contiguous_dma(reason="one value of level to a partition"):
            nc.sync.dma_start(out=level_sb[:], in_=level.rearrange("(c p) -> p c", p=P))

        v_w = [keep.tile([P, S], U32, name="v_w%d" % a, align_bytes=64) for a in range(2)]
        v_sc = keep.tile([P, S], U8, name="v_sc", align_bytes=64)

        def entries(cols):
            return slice(cols.start // 16, cols.stop // 16)

        def gather_table(a, cols):
            nc.vector.tensor_copy(v_w[a][:, cols], tab_w[a][:].bitcast(U32).indirect(idx1[:, entries(cols)]))

        def quantize(rounded, name, width, tag=None):
            codes = keep.tile([P, width], U32, name=name + "_w", tag=tag or name + "_w", align_bytes=64)
            scales = keep.tile([P, width], U8, name=name + "_sc", align_bytes=64)
            nc.vector.quantize_mx(out=codes[:].bitcast(FP8X4), scales=scales[:], in_=rounded[:])
            return codes, scales

        w1_q = {}

        def quantize_w1(a, b, vector_cols):
            rounded = keep.tile([P, PACK * PASS], BF16, name="w1_bf%d%d" % (a, b), tag="bf", bufs=4, align_bytes=64)
            dst = rounded[:].rearrange("p (t m j) -> p m j t", t=PACK, j=PACK)
            src = w1_raw[a, b][:].rearrange("p j (m t) -> p m j t", t=PACK)
            if vector_cols:
                nc.vector.tensor_copy(out=dst[:, :vector_cols], in_=src[:, :vector_cols])
                if vector_cols < P:
                    nc.scalar.copy(out=dst[:, vector_cols:], in_=src[:, vector_cols:])
            else:
                for m0 in range(0, P, P // 4):
                    nc.scalar.copy(out=dst[:, m0 : m0 + P // 4], in_=src[:, m0 : m0 + P // 4])
            w1_q[a, b] = quantize(rounded, "w1_%d%d" % (a, b), PASS)

        whole, halves = slice(0, S), [slice(0, HALF), slice(HALF, S)]
        nc.vector.tensor_copy(v_sc[:], tab_sc[:].indirect(idx1[:]))
        quantize_w1(0, 0, 0)
        quantize_w1(1, 0, 64)
        gather_table(0, whole)

        sines = [keep.tile([P, S], F32, name="sine%d" % s, tag="line%d" % s) for s in range(8)]
        wg = [keep.tile([P, S], F32, name="wg%d" % s, align_bytes=64) for s in range(8)]
        for s in range(8):
            nc.gpsimd.tensor_scalar(wg[s][:], wgs_sb[:], gain_sb[:, s // PACK, s % PACK : s % PACK + 1], 0.0, ALU.mult, ALU.add)

        taken = []

        def ring_bank(name, width):
            taken.append(name)
            bank = len(taken) % RING
            return psum.tile([P, width], F32, name=name, tag="bank%d" % bank)

        def first_stage(s, js):
            b, t = divmod(s, PACK)
            cols = slice(t * P, (t + 1) * P)
            width = js.stop - js.start
            blocks = [slice(c, c + P) for c in range(0, width, P)]
            acc = ring_bank("acc", width)
            for block in blocks:
                picked = slice(js.start + block.start, js.start + block.stop)
                for a in range(2):
                    codes, scales = w1_q[a, b]
                    nc.tensor.matmul_mx(
                        out=acc[:, block], lhsT=v_w[a][:, picked].bitcast(FP8X4), lhsT_scale=v_sc[4 * a :, picked],
                        rhs=codes[:, cols].bitcast(FP8X4), rhs_scale=scales[:, cols], start=(a == 0), stop=(a == 1),
                    )
            shifted = keep.tile([P, width], U32, name="shifted", bufs=2)
            nc.scalar.activation(shifted[:], acc[:], ACT.Copy, bias=ROUNDER, scale=1.0 / TURN)
            turns = keep.tile([P, width], F32, name="turns", bufs=2)
            nc.scalar.activation(turns[:], acc[:], ACT.Copy, bias=0.0, scale=1.0 / TURN)
            whole_turns = keep.tile([P, width], F32, name="whole_turns", bufs=2)
            nc.scalar.activation(whole_turns[:], shifted[:], ACT.Copy, bias=ROUNDER, scale=-1.0)
            rest = ring_bank("rest", width)
            for i, (term, block) in enumerate(itertools.product((turns, whole_turns), blocks)):
                nc.tensor.matmul(
                    rest[:, block], lhsT=term[:, block], rhs=ident[:], is_transpose=True,
                    start=(i == 0), stop=(i == 2 * len(blocks) - 1),
                )
            nc.scalar.activation(sines[s][:, js], rest[:], ACT.Sin, scale=TURN)

        def first_stage_head(js):
            width = js.stop - js.start
            acc = ring_bank("acc", width)
            for a in range(2):
                codes, scales = w1_q[a, 0]
                nc.tensor.matmul_mx(
                    out=acc[:], lhsT=codes[:, 0:P].bitcast(FP8X4), lhsT_scale=scales[:, 0:P],
                    rhs=v_w[a][:, js].bitcast(FP8X4), rhs_scale=v_sc[4 * a :, js], start=(a == 0), stop=(a == 1),
                )
            shifted = keep.tile([P, width], U32, name="shifted", bufs=2)
            nc.scalar.activation(shifted[:], acc[:], ACT.Copy, bias=ROUNDER, scale=1.0 / TURN)
            whole_turns = keep.tile([P, width], F32, name="whole_turns", bufs=2)
            nc.scalar.activation(whole_turns[:], shifted[:], ACT.Copy, bias=ROUNDER, scale=-1.0)
            angle = keep.tile([P, width], F32, name="angle", bufs=2)
            nc.vector.scalar_tensor_tensor(angle[:], whole_turns[:], TURN, acc[:], ALU.mult, ALU.add)
            nc.scalar.activation(sines[0][:, js], angle[:], ACT.Sin)

        th = {}

        def put(s, js):
            nc.vector.tensor_tensor(
                pages[s % 2][:].indirect(idx2[:, entries(js)]), sines[s][:, js], wg[s][:, js], ALU.mult
            )

        def fetch(s, pieces):
            b, t = divmod(s, PACK)
            width = M // pieces
            summed = keep.tile([P, M], F32, name="summed%d" % s, tag="line%d" % ((s + 1) % 8))
            for c in range(pieces):
                cols = slice(c * width, (c + 1) * width)
                nc.vector.tensor_tensor(
                    summed[:, cols],
                    pages[s % 2][:].indirect(idx3[:, c * width // 16 : (c + 1) * width // 16]),
                    tm[b][:, t, cols],
                    ALU.add,
                )
            if t == 0:
                th[b] = keep.tile([P, 2, PACK, HALF], F32, name="th%d" % b, tag="th%d" % b)
            for h in range(2):
                nc.scalar.activation(th[b][:, h, t, :], summed[:, h * HALF : (h + 1) * HALF], ACT.Tanh)

        w2_q = {}

        def quantize_w2(b):
            rounded = keep.tile([P, PACK * N], BF16, name="w2_bf%d" % b, tag="bf", bufs=4, align_bytes=64)
            nc.scalar.copy(
                out=rounded[:].rearrange("p (c i j) -> p c j i", i=4, j=PACK),
                in_=w2_raw[b][:].rearrange("p j (c i) -> p c j i", i=4),
            )
            w2_q[b] = quantize(rounded, "w2_%d" % b, N)

        z_bf, z_q = {}, {}

        def make_z(b, h):
            z = keep.tile([P, PACK * HALF], BF16, name="z%d%d" % (b, h), tag="z%d" % (h if b == 0 else 2), align_bytes=64)
            nc.vector.tensor_tensor(
                z[:].rearrange("p (c i t) -> p c t i", i=2, t=PACK),
                th[b][:, h].rearrange("p t (c i) -> p c t i", i=2),
                tm[b][:, :, h * HALF : (h + 1) * HALF].rearrange("p t (c i) -> p c t i", i=2),
                ALU.mult,
            )
            z_bf[b, h] = z

        def quantize_z(b, h, tag=None):
            z_q[b, h] = quantize(z_bf[b, h], "z_%d%d" % (b, h), HALF, tag)

        banks = {}

        def second_stage(b, h):
            z_w, z_sc = z_q[b, h]
            for c in range(N // P):
                if b == 0:
                    banks[h, c] = psum.tile([P, 2, HALF], F32, name="y%d%d" % (h, c), tag="bank%d" % (4 * h + c))
                cols = slice(c * P, (c + 1) * P)
                codes, scales = w2_q[b]
                nc.tensor.matmul_mx(
                    out=banks[h, c][:, 0, :], lhsT=codes[:, cols].bitcast(FP8X4), lhsT_scale=scales[:, cols],
                    rhs=z_w[:].bitcast(FP8X4), rhs_scale=z_sc[:], start=(b == 0), stop=False,
                )
                nc.tensor.matmul_mx(
                    out=banks[h, c][:, 1, :],
                    lhsT=w4_w[:, b, 2 * c * P : 2 * (c + 1) * P].bitcast(FP4X4), lhsT_scale=w4_sc[:, b, cols],
                    rhs=z_w[:].bitcast(FP8X4), rhs_scale=z_sc[:], start=False, stop=(b == 1),
                )

        def finish(h):
            scored = keep.tile([P, N // P, HALF], F32, name="scored%d" % h)
            best = []
            for c in range(N // P):
                y4 = keep.tile([P, HALF], F32, name="y4", bufs=8)
                nc.scalar.copy(out=y4[:], in_=banks[h, c][:, 1, :])
                larger = keep.tile([P, HALF], F32, name="larger", bufs=8)
                nc.vector.tensor_tensor(larger[:], banks[h, c][:, 0, :], y4[:], ALU.max)
                best.append(larger)
            for c, larger in enumerate(best):
                if h == 0:
                    nc.gpsimd.tensor_scalar(scored[:, c, :], larger[:], level_sb[:, c : c + 1], 0.0, ALU.mult, ALU.add)
                else:
                    nc.scalar.activation(scored[:, c, :], larger[:], ACT.Copy, scale=level_sb[:, c : c + 1])
                nc.sync.dma_start(out=out[c * P : (c + 1) * P, halves[h]], in_=scored[:, c, :])

        for h in range(2):
            gather_table(1, halves[h])
        for js in halves:
            first_stage_head(js)
        for js in halves:
            put(0, js)
        first_stage(1, whole)
        put(1, whole)
        quantize_w1(0, 1, 64)
        quantize_w1(1, 1, 0)
        for s in range(2, 8):
            first_stage(s, whole)
        fetch(0, 1)
        for s in range(2, 8):
            put(s, whole)
            if s == 7:
                for h in range(2):
                    quantize_z(0, h, ("wg7", "z0")[h])
                    second_stage(0, h)
            fetch(s - 1, 1)
            if s == 2:
                quantize_w2(0)
                quantize_w2(1)
            if s == 4:
                for h in range(2):
                    make_z(0, h)
        fetch(7, 2)
        for h in range(2):
            make_z(1, h)
            quantize_z(1, h)
            second_stage(1, h)
        for h in range(2):
            finish(h)
